import numpy as np
import ml_dtypes


def mxq(x, axis, fmt="e4m3"):
    dtype, down = {"e4m3": (ml_dtypes.float8_e4m3fn, 7), "e5m2": (ml_dtypes.float8_e5m2, 14)}[fmt]
    v = np.moveaxis(np.asarray(x, np.float32).astype(ml_dtypes.bfloat16).astype(np.float64), axis, -1)
    blocks = v.reshape(v.shape[:-1] + (-1, 32))
    amax = np.abs(blocks).max(-1, keepdims=True)
    byte = np.maximum(np.where(amax > 0, np.frexp(amax)[1] - 1 + 127, 0) - down, 1)
    scale = np.exp2(byte - 127.0)
    codes = (blocks / scale).astype(np.float32).astype(dtype).astype(np.float64)
    return np.moveaxis((codes * scale).reshape(v.shape), -1, axis)


WIDE = False


def mx_kscale(k):
    if not WIDE:
        return np.ones(k)
    levels = np.array([10, -10, 5, -5, 0])
    if k % 512:
        return np.exp2(np.random.permutation(np.resize(levels, k // 32))).repeat(32)
    a = np.empty((k // 512, 16))
    for p in range(k // 512):
        a[p, :8] = np.random.permutation(np.resize(levels, 8))
        for g in range(8):
            far = levels[np.abs(levels - a[p, g]) >= 10]
            a[p, g + 8] = far[np.random.randint(len(far))]
    return np.exp2(a.ravel()).repeat(32)


BF16 = ml_dtypes.bfloat16


def bf(x):
    return np.asarray(x, np.float32).astype(BF16)


def f64(x):
    return np.asarray(x).astype(np.float64)

def planes(Y):
    n, m = Y.shape
    b = f64(bf(Y)).reshape(n // 32, 32, m)
    amax = np.abs(b).max(1)
    byte = np.clip(np.where(amax > 0, np.frexp(amax)[1] - 1 + 127 - 7, 1), 1, 254)
    codes = (b * np.exp2(127.0 - byte)[:, None, :]).reshape(n, m).astype(np.float32).astype(ml_dtypes.float8_e4m3fn).view(np.uint8)
    words = codes.reshape(n // 512, 128, 4, m).transpose(0, 1, 3, 2)
    return np.ascontiguousarray(words), np.ascontiguousarray(byte.astype(np.uint8).reshape(n // 512, 16, m))


B, P, D, O, M = 128, 8, 512, 1024, 512


def softmax(a):
    e = np.exp(a - a.max(axis=-1, keepdims=True))
    return e / e.sum(axis=-1, keepdims=True)


def setup_inputs():
    s, t = mx_kscale(D), mx_kscale(O)
    return {
        "types": bf(np.random.standard_normal((B, P, D)) * 0.4 * s),
        "phi": bf(np.random.standard_normal((D, O)) / np.sqrt(D) / s[:, None]),
        "cost": bf(np.random.standard_normal(O) * 0.5),
        "gain": bf((1.0 + 0.1 * np.random.standard_normal(O)) * t),
        "goods": bf(np.random.standard_normal((O, M)) / np.sqrt(O) / t[:, None]),
    }


def core(types, phi, cost, gain, goods):
    num_outcomes = phi.shape[1]
    v = mxq(f64(types), 2, "e4m3") @ mxq(f64(phi), 0, "e4m3")
    w = np.sum(v, axis=1) - f64(cost)[None, :]
    p = softmax(w)
    pm = softmax(w[:, None, :] - v)
    d = num_outcomes * (pm - p[:, None, :]) * f64(gain)[None, None, :]
    return mxq(d, 2, "e4m3") @ mxq(f64(goods), 0, "e4m3")


def reference(types, phi, cost, gain, goods):
    R_out = core(types, phi, cost, gain, goods)
    words, scales = planes(np.moveaxis(R_out, 2, 0).reshape(512, -1))
    return R_out, words, scales

from contextlib import ExitStack

import concourse.mybir as mybir
from concourse.masks import make_identity

B, BIDDERS, D, O, M = 128, 8, 512, 1024, 512
FLOPS = 2 * B * BIDDERS * D * O + 2 * B * BIDDERS * O * M

F32 = mybir.dt.float32
BF16 = mybir.dt.bfloat16
U32 = mybir.dt.uint32
I32 = mybir.dt.int32
U8 = mybir.dt.uint8
FP8X4 = mybir.dt.float8_e4m3fn_x4
ALU = mybir.AluOpType
ACT = mybir.ActivationFunctionType
AX = mybir.AxisListType

P = 128
PACK = 4
GROUP = P * PACK
GROUPS = O // GROUP
PAIRS = BIDDERS // 2
LAST = BIDDERS - 1
PHI_SCALAR_COLS = 256
GOODS_PART = M // 2
PLANE_PARTS = 4
PLANE_COLS = B * BIDDERS // PLANE_PARTS
ROTATING = 4

VALUE_BANK, TURN_BANK, OUT_BANK, WORD_BANK = 0, 2, 4, 6
EARLY_VALUE_BANK = {1: WORD_BANK, 2: TURN_BANK, 4: WORD_BANK}

ORDER = """
weave_phi_vector:0 turn_types:0 spread_cost:0 copy_types:0 quant_types:0
turn_types:1 copy_types:1 turn_types:2 copy_cost:0 quant_phi:0 turn_types:3 quant_types:1
spread_cost:1 copy_types:2 copy_types:3 welfare:0:0 welfare:0:1 quant_types:2 welfare:0:2
quant_types:3 weave_phi_vector:1 weave_phi_scalar quant_phi:1 copy_cost:1 welfare:0:3 neg_welfare:0 values:0:0
sub_vector:0:0 values:1:0 weave_goods:1:0 weave_goods:1:1 half_min_w:0 welfare:1:0 half_min_first:0 welfare:1:1
welfare:1:2 welfare:1:3 quant_goods:1 values:3:0 values:2:0 copy_values:1:0 neg_welfare:1 half_min_w:1
values:0:1 sub_vector:0:1 copy_values:2:0 values:2:1 copy_values:2:1 min_w sub_vector:3:0 values:4:0 values:1:1
sub_gpsimd:1:0 values:3:1 half_min_first:1 sub_gpsimd:2:0 sub_vector:1:1 values:4:1 exp_w recip_w min_first
row_min:1 sub_gpsimd:2:1 copy_values:3:1 sub_gpsimd:3:1 row_exp:0 values:5:1 sub_vector:4:0 neg_prob:1
neg_prob:0 copy_values:4:1 copy_values:5:1 sub_gpsimd:4:1 row_recip:0
normalise:0 values:5:0 turn_neg_p:1 weave_goods:0:1 row_exp:1 sub_gpsimd:5:1 values:6:1 
copy_values:6:1 row_min:2 row_min:3 row_min:4 turn_neg_p:0 turn_pm:0:0 row_recip:1 turn_pm:0:1 sub_vector:5:0
normalise:1 apply_gain:0:0 row_exp:2 row_recip:2 row_exp:3 values:7:1 copy_values:7:1 values:6:0 
turn_neg_p:0 turn_pm:1:0 apply_gain:0:1 weave_goods:0:0 row_min:5 apply_gain:1:0 normalise:2 turn_neg_p:1
sub_vector:6:0 turn_pm:1:1 apply_gain:1:1 sub_gpsimd:6:1 row_recip:3 quant_goods:0
turn_neg_p:0 row_exp:4 quant_d:0 turn_pm:2:0 turn_neg_p:1 turn_pm:2:1 values:7:0 deliver:0:0 normalise:3
apply_gain:2:0 apply_gain:2:1 deliver:0:1 store_out:0 turn_neg_p:0 row_recip:4 turn_neg_p:1 normalise:4
round_out:0 turn_pm:3:0 sub_gpsimd:7:1 quant_d:1 quant_d:2 turn_pm:3:1 deliver:1:0 deliver:1:1 row_exp:5
round_out:1 deliver:2:0 row_min:6 apply_gain:3:0 apply_gain:3:1 sub_vector:7:0 deliver:2:1 turn_out:0
row_recip:5 normalise:5 turn_neg_p:0 turn_pm:4:0 turn_neg_p:1 turn_pm:4:1 store_out:1 turn_out:1 row_exp:6
quant_d:3 deliver:3:0 deliver:3:1 apply_gain:4:0 turn_neg_p:0 apply_gain:4:1 turn_neg_p:1 row_recip:6 quant_d:4
row_min:7 round_out:2 turn_pm:5:0 turn_pm:5:1 apply_gain:5:0 store_out:2 deliver:4:0 deliver:4:1 normalise:6
store_out:3 apply_gain:5:1 quant_d:5 turn_out:2 round_out:3 turn_out:3 turn_neg_p:0 turn_pm:6:0 row_exp:7
row_recip:7 apply_gain:6:0 copy_planes:0 normalise_half:7:0 normalise_half:7:1 store_out:4 turn_neg_p:1
turn_pm:6:1 deliver:5:0 round_out:4 deliver:5:1 turn_neg_p:0 apply_gain:6:1 quant_d:6 turn_pm:7:0 turn_neg_p:1
turn_pm:7:1 round_out:5 apply_gain:7:0 turn_out:4 apply_gain:7:1 store_out:5 turn_out:5 copy_planes:1
copy_planes:2 deliver:6:0 deliver:6:1 store_out:6 round_out:6 quant_d_half:7:0 deliver:7:0 quant_d_half:7:1
deliver:7:1 round_out:7 turn_out:6 store_out:7 turn_out:7 copy_last_planes:0 store_words:0 copy_last_planes:2
store_words:2 copy_last_planes:1 store_words:1 copy_last_planes:3 store_words:3 store_scales
"""


def tile_gibbsvcgbidderremovalallocationshift_x1_kernel(tc, types, phi, cost, gain, goods, out_0, out_1, out_2):
    nc = tc.nc
    with ExitStack() as ctx:
        keep = ctx.enter_context(tc.tile_pool(name="keep", bufs=1))
        work = ctx.enter_context(tc.tile_pool(name="work", bufs=ROTATING))
        psum = ctx.enter_context(tc.psum_pool(name="psum", bufs=1))
        ctx.enter_context(tc.manual_schedule())

        banks = [psum.tile([P, GROUP], F32, name="bank%d" % n) for n in range(8)]

        def kept(name, shape, dtype):
            return keep.tile(shape, dtype, name=name, align_bytes=64)

        def kept_list(name, count, shape, dtype):
            return [kept("%s%d" % (name, n), shape, dtype) for n in range(count)]

        ident = kept("ident", [P, P], F32)
        ident_bf = kept("ident_bf", [P, P], BF16)
        cost_col = kept("cost_col", [P, GROUPS * PACK], BF16)
        gain_col = kept("gain_col", [P, GROUPS * PACK], BF16)
        gain_1024 = kept("gain_1024", [P, GROUPS * PACK], F32)
        cost_row = kept("cost_row", [P, O], F32)
        phi_raw = kept_list("phi_raw", GROUPS, [P, PACK, GROUP], BF16)
        phi_woven = kept_list("phi_woven", GROUPS, [P, PACK * GROUP], BF16)
        phi_codes = kept("phi_codes", [P, O], U32)
        phi_scales = kept("phi_scales", [P, O], U8)
        goods_raw = kept_list("goods_raw", GROUPS, [P, PACK, M], BF16)
        goods_woven = kept_list("goods_woven", GROUPS, [P, PACK * M], BF16)
        goods_codes = kept_list("goods_codes", GROUPS, [P, M], U32)
        goods_scales = kept_list("goods_scales", GROUPS, [P, M], U8)
        types_raw = kept_list("types_raw", PAIRS, [P, 2 * D], BF16)
        types_woven = kept_list("types_woven", PAIRS, [P, 2 * B * PACK], BF16)
        types_codes = kept_list("types_codes", PAIRS, [P, 2 * B], U32)
        types_scales = kept_list("types_scales", PAIRS, [P, 2 * B], U8)
        neg_w = kept("neg_w", [P, O], F32)
        w_exp = kept("w_exp", [P, O], F32)
        neg_p = kept("neg_p", [P, O], F32)
        w_min = kept("w_min", [P, 1], F32)
        w_half_min = kept("w_half_min", [P, GROUPS], F32)
        first_half_min = kept("first_half_min", [P, GROUPS], F32)
        w_sum = kept("w_sum", [P, 1], F32)
        w_recip = kept("w_recip", [P, 1], F32)
        neg_a = kept_list("neg_a", BIDDERS, [P, O], F32)
        d_codes = kept_list("d_codes", BIDDERS, [P, GROUPS * B], U32)
        d_scales = kept_list("d_scales", BIDDERS, [P, GROUPS * B], U8)
        plane_in = kept("plane_in", [P, B * BIDDERS * PACK], BF16)
        plane_codes = kept("plane_codes", [P, B * BIDDERS], U32)
        plane_scales = kept("plane_scales", [P, B * BIDDERS], U8)
        rotating = {}

        def fresh(name, key, shape, dtype):
            rotating[name, key] = work.tile(shape, dtype, name=name, align_bytes=64)
            return rotating[name, key]

        def group_cols(g):
            return slice(g * GROUP, (g + 1) * GROUP)

        def block_cols(n):
            return slice(n * P, (n + 1) * P)

        nc.scalar.dma_start(out=cost_col[:].rearrange("p (g t) -> p g t", t=PACK), in_=cost.rearrange("(g p t) -> p g t", p=P, t=PACK))
        nc.scalar.dma_start(out=gain_col[:].rearrange("p (g t) -> p g t", t=PACK), in_=gain.rearrange("(g p t) -> p g t", p=P, t=PACK))

        def load_types(c):
            nc.sync.dma_start(out=types_raw[c][:], in_=types[:, 2 * c:2 * c + 2, :].rearrange("b i k -> b (i k)"))

        def load_phi(g):
            nc.sync.dma_start(out=phi_raw[g][:], in_=phi[:, group_cols(g)].rearrange("(p j) o -> p j o", j=PACK))

        load_types(0)
        load_types(1)
        load_phi(0)
        load_types(2)
        load_types(3)
        load_phi(1)
        for g in range(GROUPS):
            nc.sync.dma_start(out=goods_raw[g][:], in_=goods[group_cols(g), :].rearrange("(p j) m -> p j m", j=PACK))

        make_identity(nc, ident_bf[:])
        make_identity(nc, ident[:])
        nc.gpsimd.tensor_scalar(out=gain_1024[:], in0=gain_col[:], scalar1=float(O), scalar2=0.0, op0=ALU.mult, op1=ALU.add)

        def quantize(codes, scales, src):
            nc.vector.quantize_mx(out=codes.bitcast(FP8X4), scales=scales, in_=src)

        def weave(copy, dst, src, lo, hi):
            copy(
                out=dst[:, PACK * lo:PACK * hi].rearrange("p (c i j) -> p c j i", i=4, j=PACK),
                in_=src[:, :, lo:hi].rearrange("p j (c i) -> p c j i", i=4),
            )

        def in_slots(cols):
            return cols.rearrange("p (t m) -> p t m", t=PACK)

        def read_in_slots(bank):
            return bank[:].rearrange("p (m t) -> p t m", t=PACK)

        def weave_phi_vector(g):
            weave(nc.vector.tensor_copy, phi_woven[g], phi_raw[g], g * PHI_SCALAR_COLS, GROUP)

        def weave_phi_scalar():
            weave(nc.scalar.copy, phi_woven[1], phi_raw[1], 0, PHI_SCALAR_COLS)

        def quant_phi(g):
            quantize(phi_codes[:, group_cols(g)], phi_scales[:, group_cols(g)], phi_woven[g][:])

        def turn_types(c):
            words = types_raw[c][:].bitcast(F32)
            for i in range(2):
                for u in range(2):
                    nc.tensor.transpose(banks[WORD_BANK + c % 2][:, block_cols(2 * i + u)], words[:, 256 * i + u:256 * (i + 1):2], ident[:])

        def copy_types(c):
            nc.scalar.copy(
                out=types_woven[c][:].bitcast(F32).rearrange("p (i b u) -> p i b u", i=2, u=2),
                in_=banks[WORD_BANK + c % 2][:].rearrange("p (i u b) -> p i b u", i=2, u=2),
            )

        def quant_types(c):
            quantize(types_codes[c][:], types_scales[c][:], types_woven[c][:])

        def spread_cost(g):
            for t in range(PACK):
                col = PACK * g + t
                nc.tensor.matmul(out=banks[TURN_BANK + g][:, block_cols(t)], lhsT=cost_col[:, col:col + 1].to_broadcast([P, P]), rhs=ident_bf[:], start=True, stop=True)

        def copy_cost(g):
            nc.scalar.copy(out=cost_row[:, group_cols(g)], in_=banks[TURN_BANK + g][:])

        def value_pass(bank, i, g, start, stop):
            nc.tensor.matmul_mx(
                out=bank[:],
                lhsT=types_codes[i // 2][:, block_cols(i % 2)].bitcast(FP8X4),
                lhsT_scale=types_scales[i // 2][:, block_cols(i % 2)],
                rhs=phi_codes[:, group_cols(g)].bitcast(FP8X4),
                rhs_scale=phi_scales[:, group_cols(g)],
                start=start,
                stop=stop,
            )

        def welfare(g, c):
            for i in (2 * c, 2 * c + 1):
                value_pass(banks[OUT_BANK + g], i, g, i == 0, i == LAST)

        def value_bank(i, g):
            return banks[EARLY_VALUE_BANK.get(i, VALUE_BANK) + g]

        def values(i, g):
            value_pass(value_bank(i, g), i, g, True, True)

        def neg_welfare(g):
            nc.vector.tensor_tensor(out=in_slots(neg_w[:, group_cols(g)]), in0=in_slots(cost_row[:, group_cols(g)]), in1=read_in_slots(banks[OUT_BANK + g]), op=ALU.subtract)

        def minimum(dst, src):
            nc.vector.tensor_reduce(out=dst, in_=src, axis=AX.X, op=ALU.min)

        def half_min_w(g):
            minimum(w_half_min[:, g:g + 1], neg_w[:, group_cols(g)])

        def min_w():
            minimum(w_min[:], w_half_min[:])

        def exp_w():
            nc.scalar.activation(out=w_exp[:], in_=neg_w[:], func=ACT.Exp, bias=w_min[:], scale=-1.0, accum_out=w_sum[:])

        def recip_w():
            nc.vector.reciprocal(out=w_recip[:], in_=w_sum[:])

        def neg_prob(g):
            nc.vector.tensor_scalar(out=neg_p[:, group_cols(g)], in0=w_exp[:, group_cols(g)], scalar1=w_recip[:], scalar2=-1.0, op0=ALU.mult, op1=ALU.mult)

        def sub_vector(i, g):
            nc.vector.tensor_tensor(out=in_slots(neg_a[i][:, group_cols(g)]), in0=read_in_slots(value_bank(i, g)), in1=in_slots(neg_w[:, group_cols(g)]), op=ALU.add)

        def copy_values(i, g):
            nc.scalar.copy(out=in_slots(fresh("v_copy", (i, g), [P, GROUP], F32)[:]), in_=read_in_slots(value_bank(i, g)))

        def sub_gpsimd(i, g):
            nc.gpsimd.tensor_tensor(out=neg_a[i][:, group_cols(g)], in0=rotating["v_copy", (i, g)][:], in1=neg_w[:, group_cols(g)], op=ALU.add)

        def half_min_first(g):
            minimum(first_half_min[:, g:g + 1], neg_a[0][:, group_cols(g)])

        def min_first():
            minimum(fresh("a_min", 0, [P, 1], F32)[:], first_half_min[:])

        def row_min(i):
            minimum(fresh("a_min", i, [P, 1], F32)[:], neg_a[i][:])

        def row_exp(i):
            nc.scalar.activation(
                out=fresh("a_exp", i, [P, O], F32)[:], in_=neg_a[i][:], func=ACT.Exp,
                bias=rotating["a_min", i][:], scale=-1.0, accum_out=fresh("a_sum", i, [P, 1], F32)[:],
            )

        def row_recip(i):
            nc.vector.reciprocal(out=fresh("a_recip", i, [P, 1], F32)[:], in_=rotating["a_sum", i][:])

        def scale_exp(i, cols):
            nc.gpsimd.tensor_scalar(out=rotating["pm", i][:, cols], in0=rotating["a_exp", i][:, cols], scalar1=rotating["a_recip", i][:], scalar2=0.0, op0=ALU.mult, op1=ALU.add)

        def normalise(i):
            fresh("pm", i, [P, O], F32)
            scale_exp(i, slice(0, O))

        def normalise_half(i, g):
            if g == 0:
                fresh("pm", i, [P, O], F32)
            scale_exp(i, group_cols(g))

        def turn_group(src, g, opens):
            for t in range(PACK):
                nc.tensor.matmul(
                    out=banks[TURN_BANK + g][:, block_cols(t)], lhsT=src[:, block_cols(PACK * g + t)], rhs=ident[:],
                    start=opens and t == 0, stop=not opens and t == PACK - 1, is_transpose=True,
                )

        def turn_neg_p(g):
            turn_group(neg_p, g, True)

        def turn_pm(i, g):
            turn_group(rotating["pm", i], g, False)

        def apply_gain(i, g):
            if g == 0:
                fresh("d_woven", i, [P, O], BF16)
            nc.vector.tensor_tensor(
                out=rotating["d_woven", i][:, group_cols(g)].rearrange("p (b t) -> p b t", t=PACK),
                in0=banks[TURN_BANK + g][:].rearrange("p (t b) -> p b t", t=PACK),
                in1=gain_1024[:, PACK * g:PACK * (g + 1)].unsqueeze(1).to_broadcast([P, B, PACK]),
                op=ALU.mult,
            )

        def quant_d(i):
            quantize(d_codes[i][:], d_scales[i][:], rotating["d_woven", i][:])

        def quant_d_half(i, g):
            quantize(d_codes[i][:, block_cols(g)], d_scales[i][:, block_cols(g)], rotating["d_woven", i][:, group_cols(g)])

        def weave_goods(g, h):
            weave(nc.scalar.copy, goods_woven[g], goods_raw[g], h * GOODS_PART, (h + 1) * GOODS_PART)

        def quant_goods(g):
            quantize(goods_codes[g][:], goods_scales[g][:], goods_woven[g][:])

        def deliver(i, g):
            nc.tensor.matmul_mx(
                out=banks[OUT_BANK + i % 2][:],
                lhsT=d_codes[i][:, block_cols(g)].bitcast(FP8X4),
                lhsT_scale=d_scales[i][:, block_cols(g)],
                rhs=goods_codes[g][:].bitcast(FP8X4),
                rhs_scale=goods_scales[g][:],
                start=g == 0,
                stop=g == GROUPS - 1,
            )

        def store_out(i):
            result = fresh("out_f32", i, [P, M], F32)
            nc.scalar.copy(out=result[:], in_=banks[OUT_BANK + i % 2][:])
            nc.sync.dma_start(out=out_0[:, i, :], in_=result[:])

        def round_out(i):
            nc.scalar.copy(
                out=fresh("out_bf16", i, [P, M], BF16)[:].rearrange("b (u p e) -> b u p e", u=2, e=2),
                in_=banks[OUT_BANK + i % 2][:].rearrange("b (p u e) -> b u p e", u=2, e=2),
            )

        def turn_out(i):
            words = rotating["out_bf16", i][:].bitcast(F32)
            for u in range(2):
                nc.tensor.transpose(banks[WORD_BANK + (i // 2) % 2][:, block_cols(2 * (i % 2) + u)], words[:, block_cols(u)], ident[:])

        def copy_pair(c, lo, hi):
            dst = plane_in[:].bitcast(F32).rearrange("p (b q) -> p b q", q=2 * BIDDERS)
            nc.scalar.copy(out=dst[:, lo:hi, 4 * c:4 * c + 4], in_=banks[WORD_BANK + c % 2][:].rearrange("p (q b) -> p b q", q=4)[:, lo:hi, :])

        def copy_planes(c):
            copy_pair(c, 0, B)

        def copy_last_planes(h):
            copy_pair(PAIRS - 1, h * B // PLANE_PARTS, (h + 1) * B // PLANE_PARTS)

        def store_words(h):
            cols = slice(h * PLANE_COLS, (h + 1) * PLANE_COLS)
            quantize(plane_codes[:, cols], plane_scales[:, cols], plane_in[:, PACK * h * PLANE_COLS:PACK * (h + 1) * PLANE_COLS])
            nc.sync.dma_start(out=out_1[0].rearrange("p n t -> p (n t)").bitcast(I32)[:, cols], in_=plane_codes[:, cols].bitcast(I32))

        def store_scales():
            for q in range(4):
                queue = nc.scalar if q % 2 else nc.sync
                queue.dma_start(out=out_2[0].bitcast(I32)[4 * q:4 * q + 4, :], in_=plane_scales[32 * q:32 * q + 4, :].bitcast(I32))

        steps = dict(
            turn_types=turn_types, copy_types=copy_types, quant_types=quant_types,
            weave_phi_vector=weave_phi_vector, weave_phi_scalar=weave_phi_scalar, quant_phi=quant_phi, spread_cost=spread_cost,
            copy_cost=copy_cost, welfare=welfare, values=values, neg_welfare=neg_welfare, half_min_w=half_min_w, min_w=min_w,
            exp_w=exp_w, recip_w=recip_w, neg_prob=neg_prob, sub_vector=sub_vector, copy_values=copy_values, sub_gpsimd=sub_gpsimd,
            half_min_first=half_min_first, min_first=min_first, row_min=row_min, row_exp=row_exp, row_recip=row_recip,
            normalise=normalise, normalise_half=normalise_half, turn_neg_p=turn_neg_p, turn_pm=turn_pm, apply_gain=apply_gain,
            quant_d=quant_d, quant_d_half=quant_d_half, weave_goods=weave_goods, quant_goods=quant_goods, deliver=deliver,
            store_out=store_out, round_out=round_out, turn_out=turn_out, copy_planes=copy_planes,
            copy_last_planes=copy_last_planes, store_words=store_words, store_scales=store_scales,
        )
        for token in ORDER.split():
            parts = token.split(":")
            steps[parts[0]](*[int(n) for n in parts[1:]])
